import numpy as np
import ml_dtypes


def mxq(x, axis, fmt="e4m3"):
    dtype, down = {"e4m3": (ml_dtypes.float8_e4m3fn, 7), "e5m2": (ml_dtypes.float8_e5m2, 14)}[fmt]
    v = np.moveaxis(np.asarray(x, np.float32).astype(ml_dtypes.bfloat16).astype(np.float64), axis, -1)
    blocks = v.reshape(v.shape[:-1] + (-1, 32))
    amax = np.abs(blocks).max(-1, keepdims=True)
    byte = np.maximum(np.where(amax > 0, np.frexp(amax)[1] - 1 + 127, 0) - down, 1)
    scale = np.exp2(byte - 127.0)
    codes = (blocks / scale).astype(np.float32).astype(dtype).astype(np.float64)
    return np.moveaxis((codes * scale).reshape(v.shape), -1, axis)


WIDE = False


def mx_kscale(k):
    if not WIDE:
        return np.ones(k)
    levels = np.array([30, -30])
    if k % 512:
        return np.exp2(np.random.permutation(np.resize(levels, k // 32))).repeat(32)
    a = np.empty((k // 512, 16))
    for p in range(k // 512):
        a[p, :8] = np.random.permutation(np.resize(levels, 8))
        for g in range(8):
            far = levels[np.abs(levels - a[p, g]) >= 10]
            a[p, g + 8] = far[np.random.randint(len(far))]
    return np.exp2(a.ravel()).repeat(32)


def f64(x):
    return np.asarray(x).astype(np.float64)


def striped(idx):
    return np.tile(np.asarray(idx).reshape(-1, 16).T, (8, 1)).astype(np.uint16)


def unstriped(offs):
    return offs[:16].T.reshape(-1).astype(np.int64)


E2M1 = np.array([0.0, 0.5, 1.0, 1.5, 2.0, 3.0, 4.0, 6.0, -0.0, -0.5, -1.0, -1.5, -2.0, -3.0, -4.0, -6.0])


def pack_weight(w, fmt):
    k, n = w.shape
    w = f64(np.asarray(w, np.float32).astype(ml_dtypes.bfloat16)).reshape(k // 32, 32, n)
    amax = np.abs(w).max(1)
    if fmt == "e4m3":
        byte = np.frexp(amax)[1] - 1 + 127 - 7
    else:
        mant, ex = np.frexp(amax / 6.0)
        byte = np.where(mant > 0.5, ex, ex - 1) + 127
    byte = np.clip(np.where(amax > 0, byte, 1), 1, 254)
    scaled = (w * np.exp2(127.0 - byte)[:, None, :]).reshape(k, n).astype(np.float32)
    by_word = np.ascontiguousarray(scaled.reshape(k // 512, 128, 4, n).transpose(0, 1, 3, 2))
    if fmt == "e4m3":
        words = by_word.astype(ml_dtypes.float8_e4m3fn).view(np.uint8)
    else:
        c = by_word.astype(ml_dtypes.float4_e2m1fn).view(np.uint8) & 0xF
        words = (c[..., 0::2] | (c[..., 1::2] << 4)).reshape(k // 512, 128, 2 * n)
    return np.ascontiguousarray(words), np.ascontiguousarray(byte.astype(np.uint8).reshape(k // 512, 16, n))


def unpack_weight(words, scales, fmt):
    g, _, n = scales.shape
    words = np.ascontiguousarray(words).reshape(g, 128, n, -1)
    if fmt == "e4m3":
        vals = words.view(ml_dtypes.float8_e4m3fn).astype(np.float64)
    else:
        nib = np.empty((g, 128, n, 4), np.uint8)
        nib[..., 0::2] = words & 0xF
        nib[..., 1::2] = words >> 4
        vals = E2M1[nib]
    vals = vals * np.repeat(np.exp2(scales.astype(np.float64) - 127.0), 8, axis=1)[..., None]
    return vals.transpose(0, 1, 3, 2).reshape(g * 512, n)


def e4m3fn_bytes(y):
    return np.clip(np.asarray(y, np.float64), -448.0, 448.0).astype(np.float32).astype(ml_dtypes.float8_e4m3fn).view(np.uint8)


def e4m3fn_values(b):
    return np.asarray(b, np.uint8).view(ml_dtypes.float8_e4m3fn).astype(np.float64)


K, T, J, R, F, Z, N, V, O = 512, 1024, 256, 512, 512, 1024, 256, 1024, 128


def setup_inputs():
    n = np.random.standard_normal
    idx = np.random.permutation(T)[:J]
    idx2 = np.random.permutation(Z)[:J]
    idx3 = np.random.permutation(V)[:N]
    idx4 = np.random.permutation(J)[:O]
    fk = mx_kscale(K)
    ff = mx_kscale(F)
    fr = mx_kscale(R)
    xtp = pack_weight(n((K, T)) / fk[:, None], "e2m1")
    xop = pack_weight(n((F, Z)) / ff[:, None], "e4m3")
    wp = pack_weight(n((K, R)) * 1 / np.sqrt(K) * fk[:, None], "e4m3")
    w0p = pack_weight(n((F, R)) * 1 / np.sqrt(F) * ff[:, None], "e2m1")
    return {
        "xt_words": xtp[0],
        "xt_scales": xtp[1],
        "xo_words": xop[0],
        "xo_scales": xop[1],
        "w_words": wp[0],
        "w_scales": wp[1],
        "w0_words": w0p[0],
        "w0_scales": w0p[1],
        "ca": e4m3fn_bytes(60.0 * n((R, V))),
        "sw": (np.random.uniform(0.0004, 0.0012, (R, 1)) / fr[:, None]).astype(np.float32),
        "sa": (np.random.uniform(0.5, 1.6, (R, 1)) * fr[:, None]).astype(np.float32),
        "offs": striped(idx),
        "offs2": striped(idx2),
        "offs3": striped(idx3),
        "offs4": striped(idx4),
    }


def reference(xt_words, xt_scales, xo_words, xo_scales, w_words, w_scales, w0_words, w0_scales, ca, sw, sa, offs, offs2, offs3, offs4):
    idx = unstriped(offs)
    idx2 = unstriped(offs2)
    idx3 = unstriped(offs3)
    idx4 = unstriped(offs4)
    xtu = unpack_weight(xt_words, xt_scales, "e2m1")
    xou = unpack_weight(xo_words, xo_scales, "e4m3")
    wu = unpack_weight(w_words, w_scales, "e4m3")
    w0u = unpack_weight(w0_words, w0_scales, "e2m1")
    xtidxg = xtu[:, idx]
    xoidx2g = xou[:, idx2]
    a = wu.T @ xtidxg + w0u.T @ xoidx2g
    wq = e4m3fn_values(ca)[:, idx3] * f64(sw)
    g1 = np.maximum(a, 0.0)
    hid = g1[:, idx4] * f64(sa)
    wqq = mxq(wq, 0, "e4m3")
    hidq = mxq(hid, 0, "e5m2")
    p = wqq.T @ hidq
    return p

@@ -1,0 +1,173 @@
+from contextlib import ExitStack
+
+import concourse.mybir as mybir
+from concourse.masks import make_identity
+
+K, T, J, R, F, Z, N, V, O = 512, 1024, 256, 512, 512, 1024, 256, 1024, 128
+FLOPS = 2 * R * J * (K + F) + 2 * R * N * O
+
+F32 = mybir.dt.float32
+BF16 = mybir.dt.bfloat16
+I32 = mybir.dt.int32
+U32 = mybir.dt.uint32
+U16 = mybir.dt.uint16
+U8 = mybir.dt.uint8
+FP8 = mybir.dt.float8_e4m3fn
+E4M3X4 = mybir.dt.float8_e4m3fn_x4
+E5M2X4 = mybir.dt.float8_e5m2_x4
+E2M1X4 = mybir.dt.float4_e2m1fn_x4
+ACT = mybir.ActivationFunctionType
+MULT = mybir.AluOpType.mult
+
+P = 128
+PACK = 4
+RUN = 8
+BLOCKS = 16
+
+
+def tile_list_codedcolumns_kernel(tc, xt_words, xt_scales, xo_words, xo_scales, w_words, w_scales,
+                                      w0_words, w0_scales, ca, sw, sa, offs, offs2, offs3, offs4, out):
+    nc = tc.nc
+    with ExitStack() as ctx:
+        lists = ctx.enter_context(tc.tile_pool(name="lists", bufs=1))
+        sb = ctx.enter_context(tc.tile_pool(name="sb", bufs=1))
+        psum = ctx.enter_context(tc.psum_pool(name="psum", bufs=1))
+
+        idx = lists.tile([P, J // 16], U16, name="idx")
+        idx2 = lists.tile([P, J // 16], U16, name="idx2")
+        idx3 = lists.tile([P, N // 16], U16, name="idx3")
+        idx4 = lists.tile([P, O // 16], U16, name="idx4")
+
+        xo_sc = sb.tile([P, Z], U8, name="xo_sc", align_bytes=64)
+        xt_sc = sb.tile([P, T], U8, name="xt_sc", align_bytes=64)
+        xo_w = sb.tile([P, Z], U32, name="xo_w", align_bytes=64)
+        xt_w = sb.tile([P, T], U16, name="xt_w", align_bytes=64)
+        w_raw = sb.tile([P, R], U32, name="w_raw", align_bytes=64)
+        w0_raw = sb.tile([P, R // 2], U32, name="w0_raw", align_bytes=64)
+        wsc_raw = sb.tile([64, 2, R // 4], U32, name="wsc_raw", align_bytes=64)
+        w0sc_raw = sb.tile([64, 2, R // 4], U32, name="w0sc_raw", align_bytes=64)
+        ca_rows = [sb.tile([P, V], U8, name="ca_rows%d" % t, align_bytes=64) for t in range(PACK)]
+        sw_t = sb.tile([P, PACK], F32, name="sw_t")
+        sa_t = sb.tile([P, PACK], F32, name="sa_t")
+        sa_rows = sb.tile([P, P], F32, name="sa_rows")
+        sw_rows = sb.tile([P, P], F32, name="sw_rows")
+
+        nc.vector.memset(xt_sc[:].bitcast(I32), 0)
+        nc.vector.memset(wsc_raw[:].bitcast(I32), 0)
+        nc.vector.memset(xo_sc[:].bitcast(I32), 0)
+        nc.vector.memset(w0sc_raw[:].bitcast(I32), 0)
+        nc.vector.memset(sa_rows[:], 0.0)
+        nc.vector.memset(sw_rows[:], 0.0)
+
+        def load_scale_rows(queue, window, scales):
+            for quad in range(4):
+                queue.dma_start(window[32 * quad:32 * quad + 4, :].bitcast(I32),
+                                scales[0, 4 * quad:4 * quad + 4, :].bitcast(I32))
+
+        def load_weight_scale_rows(queue, raw, scales):
+            rows = scales[0].bitcast(I32).rearrange("(h c r) x -> c r h x", h=2, c=2)
+            for c in range(2):
+                queue.dma_start(raw[32 * c:32 * c + 4].bitcast(I32), rows[c])
+
+        nc.sync.dma_start(idx[:], offs)
+        nc.sync.dma_start(xt_w[:].bitcast(I32), xt_words[0].bitcast(I32))
+        load_scale_rows(nc.scalar, xt_sc, xt_scales)
+        nc.sync.dma_start(idx2[:], offs2)
+        nc.sync.dma_start(xo_w[:].bitcast(I32), xo_words[0].rearrange("p n t -> p (n t)").bitcast(I32))
+        load_weight_scale_rows(nc.gpsimd, wsc_raw, w_scales)
+        load_scale_rows(nc.sync, xo_sc, xo_scales)
+        nc.sync.dma_start(w_raw[:].bitcast(I32), w_words[0].rearrange("p n t -> p (n t)").bitcast(I32))
+        nc.sync.dma_start(w0_raw[:].bitcast(I32), w0_words[0].bitcast(I32))
+        load_weight_scale_rows(nc.sync, w0sc_raw, w0_scales)
+        nc.sync.dma_start(idx3[:], offs3)
+        ca_view = ca.rearrange("(b t q) v -> t b (q v)", t=PACK, q=RUN)
+        for t in range(PACK):
+            nc.sync.dma_start(ca_rows[t][:], ca_view[t])
+        nc.sync.dma_start(idx4[:], offs4)
+        nc.gpsimd.dma_start(sa_rows[0:PACK, :], sa.rearrange("(b t q) o -> t b (q o)", t=PACK, q=RUN))
+        nc.gpsimd.dma_start(sw_rows[0:PACK, :], sw.rearrange("(b t q) o -> t b (q o)", t=PACK, q=RUN))
+        ident = sb.tile([P, P], F32, name="ident")
+        make_identity(nc, ident[:])
+
+        xo_sc_g = sb.tile([P, J], U8, name="xo_sc_g", align_bytes=64)
+        xt_sc_g = sb.tile([P, J], U8, name="xt_sc_g", align_bytes=64)
+        xo_w_g = sb.tile([P, J], U32, name="xo_w_g", align_bytes=64)
+        xt_w_g = sb.tile([P, J], U16, name="xt_w_g", align_bytes=64)
+        nc.vector.tensor_copy(xt_w_g[:], xt_w[:].indirect(idx[:]))
+        nc.vector.tensor_copy(xt_sc_g[:], xt_sc[:].indirect(idx[:]))
+        nc.vector.tensor_copy(xo_w_g[:], xo_w[:].indirect(idx2[:]))
+        nc.vector.tensor_copy(xo_sc_g[:], xo_sc[:].indirect(idx2[:]))
+
+        def deal(dst, src):
+            nc.scalar.copy(dst.rearrange("p (t b e) -> p b t e", t=PACK, b=BLOCKS),
+                           src.rearrange("p (b t e) -> p b t e", t=PACK, b=BLOCKS))
+
+        def stationary(words_raw, scales_raw, label):
+            upper = sb.tile([64, R // 4], U32, name=label + "_upper", align_bytes=64)
+            plane = sb.tile([P, R // 4], U32, name=label + "_plane", align_bytes=64)
+            words = sb.tile(list(words_raw.shape), U32, name=label + "_words", align_bytes=64)
+            deal(upper[:], scales_raw[:, 1, :])
+            deal(plane[0:64, :], scales_raw[:, 0, :])
+            nc.vector.tensor_copy(plane[64:128, :], upper[:])
+            deal(words[:], words_raw[:])
+            return words, plane
+
+        w_st, wsc_st = stationary(w_raw, wsc_raw, "w")
+        w0_st, w0sc_st = stationary(w0_raw, w0sc_raw, "w0")
+
+        for rows, cols_t, label in ((sa_rows, sa_t, "sa_ps"), (sw_rows, sw_t, "sw_ps")):
+            turned = psum.tile([P, P], F32, name=label)
+            nc.tensor.transpose(turned[:], rows[:], ident[:])
+            nc.scalar.copy(cols_t[:], turned[:, 0:PACK])
+
+        acc = [psum.tile([P, J], F32, name="acc%d" % t) for t in range(PACK)]
+        for t in range(PACK):
+            nc.tensor.matmul_mx(acc[t][:], lhsT=w_st[:, P * t:P * t + P].bitcast(E4M3X4),
+                                lhsT_scale=wsc_st[:, 32 * t:32 * t + 32].bitcast(U8),
+                                rhs=xt_w_g[:].bitcast(E2M1X4), rhs_scale=xt_sc_g[:], start=True, stop=False)
+        for t in range(PACK):
+            nc.tensor.matmul_mx(acc[t][:], lhsT=w0_st[:, 64 * t:64 * t + 64].bitcast(E2M1X4),
+                                lhsT_scale=w0sc_st[:, 32 * t:32 * t + 32].bitcast(U8),
+                                rhs=xo_w_g[:].bitcast(E4M3X4), rhs_scale=xo_sc_g[:], start=False, stop=True)
+
+        codes = sb.tile([P, PACK, N], U8, name="codes", align_bytes=64)
+        wq = sb.tile([P, PACK, N], BF16, name="wq", align_bytes=64)
+        for t in range(PACK):
+            nc.vector.tensor_copy(codes[:, t, :], ca_rows[t][:].indirect(idx3[:]))
+        for t in range(PACK):
+            nc.vector.tensor_scalar(wq[:, t, :], codes[:, t, :].bitcast(FP8), sw_t[:, t:t + 1], None, MULT)
+
+        hid = sb.tile([P, PACK, O], BF16, name="hid", align_bytes=64)
+        for t in range(PACK):
+            g1 = sb.tile([P, J], F32, name="g1_%d" % t, align_bytes=64)
+            nc.scalar.activation(g1[:], acc[t][:], ACT.Relu)
+            nc.scalar.activation(hid[:, t, :], g1[:].indirect(idx4[:]), ACT.Copy, scale=sa_t[:, t:t + 1])
+
+        hid4 = sb.tile([P, O * PACK], BF16, name="hid4", align_bytes=64)
+        nc.scalar.copy(hid4[:].rearrange("p (c i t) -> p c t i", i=4, t=PACK),
+                       hid[:].rearrange("p t (c i) -> p c t i", i=4))
+
+        halves = range(N // P)
+        wq4 = [sb.tile([P, P * PACK], BF16, name="wq4_%d" % h, align_bytes=64) for h in halves]
+        wq_w = [sb.tile([P, P], U32, name="wq_w%d" % h, align_bytes=64) for h in halves]
+        wq_sc = [sb.tile([P, P], U8, name="wq_sc%d" % h, align_bytes=64) for h in halves]
+        for h in halves:
+            nc.vector.tensor_copy(wq4[h][:].rearrange("p (c i t) -> p c t i", i=4, t=PACK),
+                                  wq[:, :, P * h:P * h + P].rearrange("p t (c i) -> p c t i", i=4))
+        hid_w = sb.tile([P, O], U32, name="hid_w", align_bytes=64)
+        hid_sc = sb.tile([P, O], U8, name="hid_sc", align_bytes=64)
+        nc.vector.quantize_mx(wq_w[0][:].bitcast(E4M3X4), wq_sc[0][:], wq4[0][:])
+        nc.vector.quantize_mx(hid_w[:].bitcast(E5M2X4), hid_sc[:], hid4[:])
+        nc.vector.quantize_mx(wq_w[1][:].bitcast(E4M3X4), wq_sc[1][:], wq4[1][:])
+
+        for h in halves:
+            prod = psum.tile([P, O], F32, name="prod%d" % h)
+            nc.tensor.matmul_mx(prod[:], lhsT=wq_w[h][:].bitcast(E4M3X4), lhsT_scale=wq_sc[h][:],
+                                rhs=hid_w[:].bitcast(E5M2X4), rhs_scale=hid_sc[:], start=True, stop=True)
+            res = sb.tile([P, O], F32, name="res%d" % h)
+            if h == 0:
+                nc.scalar.copy(res[:], prod[:])
+                nc.scalar.dma_start(out[P * h:P * h + P, :], res[:])
+            else:
+                nc.vector.tensor_copy(res[:], prod[:])
+                nc.sync.dma_start(out[P * h:P * h + P, :], res[:])

@@ -52,40 +52,42 @@ def tile_list_codedcolumns_kernel(tc, xt_words, xt_scales, xo_words, xo_scales, 
         sa_rows = sb.tile([P, P], F32, name="sa_rows")
         sw_rows = sb.tile([P, P], F32, name="sw_rows")
 
-        nc.vector.memset(xt_sc[:].bitcast(I32), 0)
-        nc.vector.memset(wsc_raw[:].bitcast(I32), 0)
-        nc.vector.memset(xo_sc[:].bitcast(I32), 0)
-        nc.vector.memset(w0sc_raw[:].bitcast(I32), 0)
-        nc.vector.memset(sa_rows[:], 0.0)
-        nc.vector.memset(sw_rows[:], 0.0)
+        xt_raw = sb.tile([64, 2, T // 4], I32, name="xt_raw", align_bytes=64)
+        xo_raw = sb.tile([64, 2, Z // 4], I32, name="xo_raw", align_bytes=64)
+        w_planes = sb.tile([P, 2, R // 4], U32, name="w_planes", align_bytes=64)
+        w0_planes = sb.tile([P, 2, R // 4], U32, name="w0_planes", align_bytes=64)
+        nc.vector.memset(w_planes[:].bitcast(I32), 0)
+        nc.vector.memset(xt_raw[:], 0)
+        nc.gpsimd.memset(sa_rows[:], 0.0)
+        nc.vector.memset(xo_raw[:], 0)
+        nc.vector.memset(w0_planes[:].bitcast(I32), 0)
+        nc.gpsimd.memset(sw_rows[:], 0.0)
 
-        def load_scale_rows(queue, window, scales):
-            for quad in range(4):
-                queue.dma_start(window[32 * quad:32 * quad + 4, :].bitcast(I32),
-                                scales[0, 4 * quad:4 * quad + 4, :].bitcast(I32))
-
-        def load_weight_scale_rows(queue, raw, scales):
+        def load_scale_rows(queues, raw, scales):
             rows = scales[0].bitcast(I32).rearrange("(h c r) x -> c r h x", h=2, c=2)
             for c in range(2):
-                queue.dma_start(raw[32 * c:32 * c + 4].bitcast(I32), rows[c])
+                queues[c].dma_start(raw[32 * c:32 * c + 4].bitcast(I32), rows[c])
 
+        on_sync = (nc.sync, nc.sync)
         nc.sync.dma_start(idx[:], offs)
         nc.sync.dma_start(xt_w[:].bitcast(I32), xt_words[0].bitcast(I32))
-        load_scale_rows(nc.scalar, xt_sc, xt_scales)
         nc.sync.dma_start(idx2[:], offs2)
+        load_scale_rows(on_sync, wsc_raw, w_scales)
+        load_scale_rows((nc.scalar, nc.sync), xt_raw, xt_scales)
         nc.sync.dma_start(xo_w[:].bitcast(I32), xo_words[0].rearrange("p n t -> p (n t)").bitcast(I32))
-        load_weight_scale_rows(nc.gpsimd, wsc_raw, w_scales)
-        load_scale_rows(nc.sync, xo_sc, xo_scales)
         nc.sync.dma_start(w_raw[:].bitcast(I32), w_words[0].rearrange("p n t -> p (n t)").bitcast(I32))
+        load_scale_rows(on_sync, xo_raw, xo_scales)
         nc.sync.dma_start(w0_raw[:].bitcast(I32), w0_words[0].bitcast(I32))
-        load_weight_scale_rows(nc.sync, w0sc_raw, w0_scales)
+        load_scale_rows(on_sync, w0sc_raw, w0_scales)
         nc.sync.dma_start(idx3[:], offs3)
         ca_view = ca.rearrange("(b t q) v -> t b (q v)", t=PACK, q=RUN)
-        for t in range(PACK):
+        for t in range(2):
             nc.sync.dma_start(ca_rows[t][:], ca_view[t])
+        nc.sync.dma_start(sa_rows[0:PACK, :], sa.rearrange("(b t q) o -> t b (q o)", t=PACK, q=RUN))
+        nc.sync.dma_start(ca_rows[2][:], ca_view[2])
         nc.sync.dma_start(idx4[:], offs4)
-        nc.gpsimd.dma_start(sa_rows[0:PACK, :], sa.rearrange("(b t q) o -> t b (q o)", t=PACK, q=RUN))
-        nc.gpsimd.dma_start(sw_rows[0:PACK, :], sw.rearrange("(b t q) o -> t b (q o)", t=PACK, q=RUN))
+        nc.sync.dma_start(ca_rows[3][:], ca_view[3])
+        nc.sync.dma_start(sw_rows[0:PACK, :], sw.rearrange("(b t q) o -> t b (q o)", t=PACK, q=RUN))
         ident = sb.tile([P, P], F32, name="ident")
         make_identity(nc, ident[:])
 
@@ -93,42 +95,48 @@ def tile_list_codedcolumns_kernel(tc, xt_words, xt_scales, xo_words, xo_scales, 
         xt_sc_g = sb.tile([P, J], U8, name="xt_sc_g", align_bytes=64)
         xo_w_g = sb.tile([P, J], U32, name="xo_w_g", align_bytes=64)
         xt_w_g = sb.tile([P, J], U16, name="xt_w_g", align_bytes=64)
-        nc.vector.tensor_copy(xt_w_g[:], xt_w[:].indirect(idx[:]))
+        def spread(window, raw):
+            for h in range(2):
+                nc.vector.tensor_copy(window[64 * h:64 * h + 64, :].bitcast(I32), raw[:, h, :])
+
+        spread(xt_sc, xt_raw)
         nc.vector.tensor_copy(xt_sc_g[:], xt_sc[:].indirect(idx[:]))
+        nc.vector.tensor_copy(xt_w_g[:], xt_w[:].indirect(idx[:]))
         nc.vector.tensor_copy(xo_w_g[:], xo_w[:].indirect(idx2[:]))
+        spread(xo_sc, xo_raw)
         nc.vector.tensor_copy(xo_sc_g[:], xo_sc[:].indirect(idx2[:]))
 
-        def deal(dst, src):
-            nc.scalar.copy(dst.rearrange("p (t b e) -> p b t e", t=PACK, b=BLOCKS),
-                           src.rearrange("p (b t e) -> p b t e", t=PACK, b=BLOCKS))
+        def stationary(words_raw, scales_raw, planes, label):
+            words = sb.tile(list(words_raw.shape), U32, name=label, align_bytes=64)
+            for c in range(2):
+                rows = slice(32 * c, 32 * c + 4)
+                nc.scalar.copy(planes[rows].rearrange("p h (t b e) -> p h b t e", t=PACK, b=BLOCKS),
+                               scales_raw[rows].rearrange("p h (b t e) -> p h b t e", t=PACK, b=BLOCKS))
+            nc.vector.tensor_copy(planes[64:128, 0, :], planes[0:64, 1, :])
+            nc.scalar.copy(words[:].rearrange("p (t b e) -> p b t e", t=PACK, b=BLOCKS),
+                           words_raw[:].rearrange("p (b t e) -> p b t e", t=PACK, b=BLOCKS))
+            return words
 
-        def stationary(words_raw, scales_raw, label):
-            upper = sb.tile([64, R // 4], U32, name=label + "_upper", align_bytes=64)
-            plane = sb.tile([P, R // 4], U32, name=label + "_plane", align_bytes=64)
-            words = sb.tile(list(words_raw.shape), U32, name=label + "_words", align_bytes=64)
-            deal(upper[:], scales_raw[:, 1, :])
-            deal(plane[0:64, :], scales_raw[:, 0, :])
-            nc.vector.tensor_copy(plane[64:128, :], upper[:])
-            deal(words[:], words_raw[:])
-            return words, plane
-
-        w_st, wsc_st = stationary(w_raw, wsc_raw, "w")
-        w0_st, w0sc_st = stationary(w0_raw, w0sc_raw, "w0")
-
-        for rows, cols_t, label in ((sa_rows, sa_t, "sa_ps"), (sw_rows, sw_t, "sw_ps")):
+        def turn(rows, columns, label):
             turned = psum.tile([P, P], F32, name=label)
             nc.tensor.transpose(turned[:], rows[:], ident[:])
-            nc.scalar.copy(cols_t[:], turned[:, 0:PACK])
+            nc.scalar.copy(columns[:], turned[:, 0:PACK])
+
+        w_st = stationary(w_raw, wsc_raw, w_planes, "w_st")
+        w0_st = stationary(w0_raw, w0sc_raw, w0_planes, "w0_st")
 
         acc = [psum.tile([P, J], F32, name="acc%d" % t) for t in range(PACK)]
         for t in range(PACK):
             nc.tensor.matmul_mx(acc[t][:], lhsT=w_st[:, P * t:P * t + P].bitcast(E4M3X4),
-                                lhsT_scale=wsc_st[:, 32 * t:32 * t + 32].bitcast(U8),
+                                lhsT_scale=w_planes[:, 0, 32 * t:32 * t + 32].bitcast(U8),
                                 rhs=xt_w_g[:].bitcast(E2M1X4), rhs_scale=xt_sc_g[:], start=True, stop=False)
         for t in range(PACK):
             nc.tensor.matmul_mx(acc[t][:], lhsT=w0_st[:, 64 * t:64 * t + 64].bitcast(E2M1X4),
-                                lhsT_scale=w0sc_st[:, 32 * t:32 * t + 32].bitcast(U8),
+                                lhsT_scale=w0_planes[:, 0, 32 * t:32 * t + 32].bitcast(U8),
                                 rhs=xo_w_g[:].bitcast(E4M3X4), rhs_scale=xo_sc_g[:], start=False, stop=True)
+
+        turn(sa_rows, sa_t, "sa_ps")
+        turn(sw_rows, sw_t, "sw_ps")
 
         codes = sb.tile([P, PACK, N], U8, name="codes", align_bytes=64)
         wq = sb.tile([P, PACK, N], BF16, name="wq", align_bytes=64)
@@ -138,10 +146,11 @@ def tile_list_codedcolumns_kernel(tc, xt_words, xt_scales, xo_words, xo_scales, 
             nc.vector.tensor_scalar(wq[:, t, :], codes[:, t, :].bitcast(FP8), sw_t[:, t:t + 1], None, MULT)
 
         hid = sb.tile([P, PACK, O], BF16, name="hid", align_bytes=64)
+        g1 = [sb.tile([P, J], F32, name="g1_%d" % t, align_bytes=64) for t in range(PACK)]
         for t in range(PACK):
-            g1 = sb.tile([P, J], F32, name="g1_%d" % t, align_bytes=64)
-            nc.scalar.activation(g1[:], acc[t][:], ACT.Relu)
-            nc.scalar.activation(hid[:, t, :], g1[:].indirect(idx4[:]), ACT.Copy, scale=sa_t[:, t:t + 1])
+            nc.scalar.activation(g1[t][:], acc[t][:], ACT.Relu)
+        for t in range(PACK):
+            nc.scalar.activation(hid[:, t, :], g1[t][:].indirect(idx4[:]), ACT.Copy, scale=sa_t[:, t:t + 1])
 
         hid4 = sb.tile([P, O * PACK], BF16, name="hid4", align_bytes=64)
         nc.scalar.copy(hid4[:].rearrange("p (c i t) -> p c t i", i=4, t=PACK),

@@ -44,7 +44,7 @@ def tile_list_codedcolumns_kernel(tc, xt_words, xt_scales, xo_words, xo_scales, 
         xt_w = sb.tile([P, T], U16, name="xt_w", align_bytes=64)
         w_raw = sb.tile([P, R], U32, name="w_raw", align_bytes=64)
         w0_raw = sb.tile([P, R // 2], U32, name="w0_raw", align_bytes=64)
-        wsc_raw = sb.tile([64, 2, R // 4], U32, name="wsc_raw", align_bytes=64)
+        wsc_raw = sb.tile([4, 4, R // 4], I32, name="wsc_raw", align_bytes=64)
         w0sc_raw = sb.tile([64, 2, R // 4], U32, name="w0sc_raw", align_bytes=64)
         ca_rows = [sb.tile([P, V], U8, name="ca_rows%d" % t, align_bytes=64) for t in range(PACK)]
         sw_t = sb.tile([P, PACK], F32, name="sw_t")
@@ -54,42 +54,42 @@ def tile_list_codedcolumns_kernel(tc, xt_words, xt_scales, xo_words, xo_scales, 
 
         xt_raw = sb.tile([64, 2, T // 4], I32, name="xt_raw", align_bytes=64)
         xo_raw = sb.tile([64, 2, Z // 4], I32, name="xo_raw", align_bytes=64)
-        w_planes = sb.tile([P, 2, R // 4], U32, name="w_planes", align_bytes=64)
+        w_plane = sb.tile([P, R // 4], I32, name="w_plane", align_bytes=64)
         w0_planes = sb.tile([P, 2, R // 4], U32, name="w0_planes", align_bytes=64)
-        nc.vector.memset(w_planes[:].bitcast(I32), 0)
+        ident = sb.tile([P, P], F32, name="ident")
         nc.vector.memset(xt_raw[:], 0)
-        nc.gpsimd.memset(sa_rows[:], 0.0)
         nc.vector.memset(xo_raw[:], 0)
+        nc.vector.memset(w_plane[:], 0)
         nc.vector.memset(w0_planes[:].bitcast(I32), 0)
-        nc.gpsimd.memset(sw_rows[:], 0.0)
+        nc.vector.memset(sa_rows[:], 0.0)
+        nc.vector.memset(sw_rows[:], 0.0)
+        nc.vector.memset(ident[:], 0.0)
+        make_identity(nc, ident[:], nomemset=True)
 
-        def load_scale_rows(queues, raw, scales):
+        def load_scale_rows(raw, scales):
             rows = scales[0].bitcast(I32).rearrange("(h c r) x -> c r h x", h=2, c=2)
             for c in range(2):
-                queues[c].dma_start(raw[32 * c:32 * c + 4].bitcast(I32), rows[c])
+                nc.sync.dma_start(raw[32 * c:32 * c + 4].bitcast(I32), rows[c])
 
-        on_sync = (nc.sync, nc.sync)
         nc.sync.dma_start(idx[:], offs)
         nc.sync.dma_start(xt_w[:].bitcast(I32), xt_words[0].bitcast(I32))
         nc.sync.dma_start(idx2[:], offs2)
-        load_scale_rows(on_sync, wsc_raw, w_scales)
-        load_scale_rows((nc.scalar, nc.sync), xt_raw, xt_scales)
-        nc.sync.dma_start(xo_w[:].bitcast(I32), xo_words[0].rearrange("p n t -> p (n t)").bitcast(I32))
+        nc.sync.dma_start(wsc_raw[:], w_scales[0].bitcast(I32).rearrange("(quad r) x -> r quad x", r=4))
+        load_scale_rows(xt_raw, xt_scales)
         nc.sync.dma_start(w_raw[:].bitcast(I32), w_words[0].rearrange("p n t -> p (n t)").bitcast(I32))
-        load_scale_rows(on_sync, xo_raw, xo_scales)
+        nc.sync.dma_start(xo_w[:].bitcast(I32), xo_words[0].rearrange("p n t -> p (n t)").bitcast(I32))
+        load_scale_rows(xo_raw, xo_scales)
         nc.sync.dma_start(w0_raw[:].bitcast(I32), w0_words[0].bitcast(I32))
-        load_scale_rows(on_sync, w0sc_raw, w0_scales)
+        load_scale_rows(w0sc_raw, w0_scales)
         nc.sync.dma_start(idx3[:], offs3)
         ca_view = ca.rearrange("(b t q) v -> t b (q v)", t=PACK, q=RUN)
         for t in range(2):
             nc.sync.dma_start(ca_rows[t][:], ca_view[t])
         nc.sync.dma_start(sa_rows[0:PACK, :], sa.rearrange("(b t q) o -> t b (q o)", t=PACK, q=RUN))
         nc.sync.dma_start(ca_rows[2][:], ca_view[2])
-        nc.sync.dma_start(idx4[:], offs4)
         nc.sync.dma_start(ca_rows[3][:], ca_view[3])
         nc.sync.dma_start(sw_rows[0:PACK, :], sw.rearrange("(b t q) o -> t b (q o)", t=PACK, q=RUN))
-        ident = sb.tile([P, P], F32, name="ident")
-        make_identity(nc, ident[:])
+        nc.sync.dma_start(idx4[:], offs4)
 
         xo_sc_g = sb.tile([P, J], U8, name="xo_sc_g", align_bytes=64)
         xt_sc_g = sb.tile([P, J], U8, name="xt_sc_g", align_bytes=64)
@@ -99,44 +99,47 @@ def tile_list_codedcolumns_kernel(tc, xt_words, xt_scales, xo_words, xo_scales, 
             for h in range(2):
                 nc.vector.tensor_copy(window[64 * h:64 * h + 64, :].bitcast(I32), raw[:, h, :])
 
+        nc.vector.tensor_copy(xt_w_g[:], xt_w[:].indirect(idx[:]))
         spread(xt_sc, xt_raw)
         nc.vector.tensor_copy(xt_sc_g[:], xt_sc[:].indirect(idx[:]))
-        nc.vector.tensor_copy(xt_w_g[:], xt_w[:].indirect(idx[:]))
+        for quad in range(4):
+            nc.vector.tensor_copy(w_plane[32 * quad:32 * quad + 4, :].rearrange("p (t b e) -> p t b e", t=PACK, b=BLOCKS),
+                                  wsc_raw[:, quad, :].rearrange("p (b t e) -> p t b e", t=PACK, b=BLOCKS))
         nc.vector.tensor_copy(xo_w_g[:], xo_w[:].indirect(idx2[:]))
         spread(xo_sc, xo_raw)
         nc.vector.tensor_copy(xo_sc_g[:], xo_sc[:].indirect(idx2[:]))
 
-        def stationary(words_raw, scales_raw, planes, label):
+        def deal_words(words_raw, label):
             words = sb.tile(list(words_raw.shape), U32, name=label, align_bytes=64)
-            for c in range(2):
-                rows = slice(32 * c, 32 * c + 4)
-                nc.scalar.copy(planes[rows].rearrange("p h (t b e) -> p h b t e", t=PACK, b=BLOCKS),
-                               scales_raw[rows].rearrange("p h (b t e) -> p h b t e", t=PACK, b=BLOCKS))
-            nc.vector.tensor_copy(planes[64:128, 0, :], planes[0:64, 1, :])
-            nc.scalar.copy(words[:].rearrange("p (t b e) -> p b t e", t=PACK, b=BLOCKS),
-                           words_raw[:].rearrange("p (b t e) -> p b t e", t=PACK, b=BLOCKS))
+            nc.scalar.copy(words[:].rearrange("p (t b e) -> p t b e", t=PACK, b=BLOCKS),
+                           words_raw[:].rearrange("p (b t e) -> p t b e", t=PACK, b=BLOCKS))
             return words
 
-        def turn(rows, columns, label):
+        w_st = deal_words(w_raw, "w_st")
+        for c in range(2):
+            rows = slice(32 * c, 32 * c + 4)
+            nc.scalar.copy(w0_planes[rows].rearrange("p h (t b e) -> p h b t e", t=PACK, b=BLOCKS),
+                           w0sc_raw[rows].rearrange("p h (b t e) -> p h b t e", t=PACK, b=BLOCKS))
+        nc.vector.tensor_copy(w0_planes[64:128, 0, :], w0_planes[0:64, 1, :])
+        w0_st = deal_words(w0_raw, "w0_st")
+
+        def turn(rows, columns, label, copy_out):
             turned = psum.tile([P, P], F32, name=label)
             nc.tensor.transpose(turned[:], rows[:], ident[:])
-            nc.scalar.copy(columns[:], turned[:, 0:PACK])
-
-        w_st = stationary(w_raw, wsc_raw, w_planes, "w_st")
-        w0_st = stationary(w0_raw, w0sc_raw, w0_planes, "w0_st")
+            copy_out(columns[:], turned[:, 0:PACK])
 
         acc = [psum.tile([P, J], F32, name="acc%d" % t) for t in range(PACK)]
         for t in range(PACK):
             nc.tensor.matmul_mx(acc[t][:], lhsT=w_st[:, P * t:P * t + P].bitcast(E4M3X4),
-                                lhsT_scale=w_planes[:, 0, 32 * t:32 * t + 32].bitcast(U8),
+                                lhsT_scale=w_plane[:, 32 * t:32 * t + 32].bitcast(U8),
                                 rhs=xt_w_g[:].bitcast(E2M1X4), rhs_scale=xt_sc_g[:], start=True, stop=False)
         for t in range(PACK):
             nc.tensor.matmul_mx(acc[t][:], lhsT=w0_st[:, 64 * t:64 * t + 64].bitcast(E2M1X4),
                                 lhsT_scale=w0_planes[:, 0, 32 * t:32 * t + 32].bitcast(U8),
                                 rhs=xo_w_g[:].bitcast(E4M3X4), rhs_scale=xo_sc_g[:], start=False, stop=True)
 
-        turn(sa_rows, sa_t, "sa_ps")
-        turn(sw_rows, sw_t, "sw_ps")
+        turn(sa_rows, sa_t, "sa_ps", nc.scalar.copy)
+        turn(sw_rows, sw_t, "sw_ps", nc.vector.tensor_copy)
 
         codes = sb.tile([P, PACK, N], U8, name="codes", align_bytes=64)
         wq = sb.tile([P, PACK, N], BF16, name="wq", align_bytes=64)
@@ -153,21 +156,24 @@ def tile_list_codedcolumns_kernel(tc, xt_words, xt_scales, xo_words, xo_scales, 
             nc.scalar.activation(hid[:, t, :], g1[t][:].indirect(idx4[:]), ACT.Copy, scale=sa_t[:, t:t + 1])
 
         hid4 = sb.tile([P, O * PACK], BF16, name="hid4", align_bytes=64)
-        nc.scalar.copy(hid4[:].rearrange("p (c i t) -> p c t i", i=4, t=PACK),
-                       hid[:].rearrange("p t (c i) -> p c t i", i=4))
+
+        def weave(copy, dst, src):
+            copy(dst.rearrange("p (c i t) -> p c t i", i=4, t=PACK), src.rearrange("p t (c i) -> p c t i", i=4))
+
+        weave(nc.scalar.copy, hid4[:, 0:O * PACK // 2], hid[:, :, 0:O // 2])
 
         halves = range(N // P)
         wq4 = [sb.tile([P, P * PACK], BF16, name="wq4_%d" % h, align_bytes=64) for h in halves]
         wq_w = [sb.tile([P, P], U32, name="wq_w%d" % h, align_bytes=64) for h in halves]
         wq_sc = [sb.tile([P, P], U8, name="wq_sc%d" % h, align_bytes=64) for h in halves]
         for h in halves:
-            nc.vector.tensor_copy(wq4[h][:].rearrange("p (c i t) -> p c t i", i=4, t=PACK),
-                                  wq[:, :, P * h:P * h + P].rearrange("p t (c i) -> p c t i", i=4))
+            weave(nc.vector.tensor_copy, wq4[h][:], wq[:, :, P * h:P * h + P])
+        for h in halves:
+            nc.vector.quantize_mx(wq_w[h][:].bitcast(E4M3X4), wq_sc[h][:], wq4[h][:])
+        weave(nc.vector.tensor_copy, hid4[:, O * PACK // 2:], hid[:, :, O // 2:])
         hid_w = sb.tile([P, O], U32, name="hid_w", align_bytes=64)
         hid_sc = sb.tile([P, O], U8, name="hid_sc", align_bytes=64)
-        nc.vector.quantize_mx(wq_w[0][:].bitcast(E4M3X4), wq_sc[0][:], wq4[0][:])
         nc.vector.quantize_mx(hid_w[:].bitcast(E5M2X4), hid_sc[:], hid4[:])
-        nc.vector.quantize_mx(wq_w[1][:].bitcast(E4M3X4), wq_sc[1][:], wq4[1][:])
 
         for h in halves:
             prod = psum.tile([P, O], F32, name="prod%d" % h)

@@ -20,9 +20,15 @@ ACT = mybir.ActivationFunctionType
 MULT = mybir.AluOpType.mult
 
 P = 128
+HALF = P // 2
+QUAD = 32
+LIVE = 4
 PACK = 4
 RUN = 8
-BLOCKS = 16
+BLOCKS = R // (PACK * RUN)
+LIST_ROWS = 16
+BYTES_PER_I32 = 4
+WEAVE = 4
 
 
 def tile_list_codedcolumns_kernel(tc, xt_words, xt_scales, xo_words, xo_scales, w_words, w_scales,
@@ -33,10 +39,10 @@ def tile_list_codedcolumns_kernel(tc, xt_words, xt_scales, xo_words, xo_scales, 
         sb = ctx.enter_context(tc.tile_pool(name="sb", bufs=1))
         psum = ctx.enter_context(tc.psum_pool(name="psum", bufs=1))
 
-        idx = lists.tile([P, J // 16], U16, name="idx")
-        idx2 = lists.tile([P, J // 16], U16, name="idx2")
-        idx3 = lists.tile([P, N // 16], U16, name="idx3")
-        idx4 = lists.tile([P, O // 16], U16, name="idx4")
+        idx = lists.tile([P, J // LIST_ROWS], U16, name="idx")
+        idx2 = lists.tile([P, J // LIST_ROWS], U16, name="idx2")
+        idx3 = lists.tile([P, N // LIST_ROWS], U16, name="idx3")
+        idx4 = lists.tile([P, O // LIST_ROWS], U16, name="idx4")
 
         xo_sc = sb.tile([P, Z], U8, name="xo_sc", align_bytes=64)
         xt_sc = sb.tile([P, T], U8, name="xt_sc", align_bytes=64)
@@ -44,50 +50,51 @@ def tile_list_codedcolumns_kernel(tc, xt_words, xt_scales, xo_words, xo_scales, 
         xt_w = sb.tile([P, T], U16, name="xt_w", align_bytes=64)
         w_raw = sb.tile([P, R], U32, name="w_raw", align_bytes=64)
         w0_raw = sb.tile([P, R // 2], U32, name="w0_raw", align_bytes=64)
-        wsc_raw = sb.tile([4, 4, R // 4], I32, name="wsc_raw", align_bytes=64)
-        w0sc_raw = sb.tile([64, 2, R // 4], U32, name="w0sc_raw", align_bytes=64)
+        wsc_raw = sb.tile([LIVE, 4, R // BYTES_PER_I32], I32, name="wsc_raw", align_bytes=64)
+        w0sc_raw = sb.tile([HALF, 2, R // BYTES_PER_I32], U32, name="w0sc_raw", align_bytes=64)
         ca_rows = [sb.tile([P, V], U8, name="ca_rows%d" % t, align_bytes=64) for t in range(PACK)]
         sw_t = sb.tile([P, PACK], F32, name="sw_t")
         sa_t = sb.tile([P, PACK], F32, name="sa_t")
         sa_rows = sb.tile([P, P], F32, name="sa_rows")
         sw_rows = sb.tile([P, P], F32, name="sw_rows")
 
-        xt_raw = sb.tile([64, 2, T // 4], I32, name="xt_raw", align_bytes=64)
-        xo_raw = sb.tile([64, 2, Z // 4], I32, name="xo_raw", align_bytes=64)
-        w_plane = sb.tile([P, R // 4], I32, name="w_plane", align_bytes=64)
-        w0_planes = sb.tile([P, 2, R // 4], U32, name="w0_planes", align_bytes=64)
+        xt_raw = sb.tile([HALF, 2, T // BYTES_PER_I32], I32, name="xt_raw", align_bytes=64)
+        xo_raw = sb.tile([HALF, 2, Z // BYTES_PER_I32], I32, name="xo_raw", align_bytes=64)
+        w_sc = sb.tile([P, R // BYTES_PER_I32], I32, name="w_sc", align_bytes=64)
+        w0_sc = sb.tile([P, 2, R // BYTES_PER_I32], U32, name="w0_sc", align_bytes=64)
         ident = sb.tile([P, P], F32, name="ident")
+
         nc.vector.memset(xt_raw[:], 0)
         nc.vector.memset(xo_raw[:], 0)
-        nc.vector.memset(w_plane[:], 0)
-        nc.vector.memset(w0_planes[:].bitcast(I32), 0)
+        nc.vector.memset(w_sc[:], 0)
+        nc.vector.memset(w0_sc[:].bitcast(I32), 0)
         nc.vector.memset(sa_rows[:], 0.0)
         nc.vector.memset(sw_rows[:], 0.0)
         nc.vector.memset(ident[:], 0.0)
         make_identity(nc, ident[:], nomemset=True)
 
         def load_scale_rows(raw, scales):
-            rows = scales[0].bitcast(I32).rearrange("(h c r) x -> c r h x", h=2, c=2)
+            rows = scales[0].bitcast(I32).rearrange("(h c i) x -> c i h x", h=2, c=2)
             for c in range(2):
-                nc.sync.dma_start(raw[32 * c:32 * c + 4].bitcast(I32), rows[c])
+                nc.sync.dma_start(raw[QUAD * c:QUAD * c + LIVE].bitcast(I32), rows[c])
 
         nc.sync.dma_start(idx[:], offs)
         nc.sync.dma_start(xt_w[:].bitcast(I32), xt_words[0].bitcast(I32))
         nc.sync.dma_start(idx2[:], offs2)
-        nc.sync.dma_start(wsc_raw[:], w_scales[0].bitcast(I32).rearrange("(quad r) x -> r quad x", r=4))
+        nc.sync.dma_start(wsc_raw[:], w_scales[0].bitcast(I32).rearrange("(quad i) x -> i quad x", i=LIVE))
         load_scale_rows(xt_raw, xt_scales)
-        nc.sync.dma_start(w_raw[:].bitcast(I32), w_words[0].rearrange("p n t -> p (n t)").bitcast(I32))
         nc.sync.dma_start(xo_w[:].bitcast(I32), xo_words[0].rearrange("p n t -> p (n t)").bitcast(I32))
+        nc.sync.dma_start(w_raw[:].bitcast(I32), w_words[0].rearrange("p n t -> p (n t)").bitcast(I32))
         load_scale_rows(xo_raw, xo_scales)
         nc.sync.dma_start(w0_raw[:].bitcast(I32), w0_words[0].bitcast(I32))
         load_scale_rows(w0sc_raw, w0_scales)
         nc.sync.dma_start(idx3[:], offs3)
-        ca_view = ca.rearrange("(b t q) v -> t b (q v)", t=PACK, q=RUN)
-        for t in range(2):
-            nc.sync.dma_start(ca_rows[t][:], ca_view[t])
+        ca_planes = ca.rearrange("(b t q) v -> t b (q v)", t=PACK, q=RUN)
+        for t in range(PACK // 2):
+            nc.sync.dma_start(ca_rows[t][:], ca_planes[t])
         nc.sync.dma_start(sa_rows[0:PACK, :], sa.rearrange("(b t q) o -> t b (q o)", t=PACK, q=RUN))
-        nc.sync.dma_start(ca_rows[2][:], ca_view[2])
-        nc.sync.dma_start(ca_rows[3][:], ca_view[3])
+        for t in range(PACK // 2, PACK):
+            nc.sync.dma_start(ca_rows[t][:], ca_planes[t])
         nc.sync.dma_start(sw_rows[0:PACK, :], sw.rearrange("(b t q) o -> t b (q o)", t=PACK, q=RUN))
         nc.sync.dma_start(idx4[:], offs4)
 
@@ -95,16 +102,18 @@ def tile_list_codedcolumns_kernel(tc, xt_words, xt_scales, xo_words, xo_scales, 
         xt_sc_g = sb.tile([P, J], U8, name="xt_sc_g", align_bytes=64)
         xo_w_g = sb.tile([P, J], U32, name="xo_w_g", align_bytes=64)
         xt_w_g = sb.tile([P, J], U16, name="xt_w_g", align_bytes=64)
+
         def spread(window, raw):
             for h in range(2):
-                nc.vector.tensor_copy(window[64 * h:64 * h + 64, :].bitcast(I32), raw[:, h, :])
+                nc.vector.tensor_copy(window[HALF * h:HALF * h + HALF, :].bitcast(I32), raw[:, h, :])
 
         nc.vector.tensor_copy(xt_w_g[:], xt_w[:].indirect(idx[:]))
         spread(xt_sc, xt_raw)
         nc.vector.tensor_copy(xt_sc_g[:], xt_sc[:].indirect(idx[:]))
-        for quad in range(4):
-            nc.vector.tensor_copy(w_plane[32 * quad:32 * quad + 4, :].rearrange("p (t b e) -> p t b e", t=PACK, b=BLOCKS),
-                                  wsc_raw[:, quad, :].rearrange("p (b t e) -> p t b e", t=PACK, b=BLOCKS))
+        for quad in range(P // QUAD):
+            nc.vector.tensor_copy(
+                w_sc[QUAD * quad:QUAD * quad + LIVE, :].rearrange("p (t b e) -> p t b e", t=PACK, b=BLOCKS),
+                wsc_raw[:, quad, :].rearrange("p (b t e) -> p t b e", t=PACK, b=BLOCKS))
         nc.vector.tensor_copy(xo_w_g[:], xo_w[:].indirect(idx2[:]))
         spread(xo_sc, xo_raw)
         nc.vector.tensor_copy(xo_sc_g[:], xo_sc[:].indirect(idx2[:]))
@@ -117,10 +126,10 @@ def tile_list_codedcolumns_kernel(tc, xt_words, xt_scales, xo_words, xo_scales, 
 
         w_st = deal_words(w_raw, "w_st")
         for c in range(2):
-            rows = slice(32 * c, 32 * c + 4)
-            nc.scalar.copy(w0_planes[rows].rearrange("p h (t b e) -> p h b t e", t=PACK, b=BLOCKS),
+            rows = slice(QUAD * c, QUAD * c + LIVE)
+            nc.scalar.copy(w0_sc[rows].rearrange("p h (t b e) -> p h b t e", t=PACK, b=BLOCKS),
                            w0sc_raw[rows].rearrange("p h (b t e) -> p h b t e", t=PACK, b=BLOCKS))
-        nc.vector.tensor_copy(w0_planes[64:128, 0, :], w0_planes[0:64, 1, :])
+        nc.vector.tensor_copy(w0_sc[HALF:P, 0, :], w0_sc[0:HALF, 1, :])
         w0_st = deal_words(w0_raw, "w0_st")
 
         def turn(rows, columns, label, copy_out):
@@ -129,13 +138,14 @@ def tile_list_codedcolumns_kernel(tc, xt_words, xt_scales, xo_words, xo_scales, 
             copy_out(columns[:], turned[:, 0:PACK])
 
         acc = [psum.tile([P, J], F32, name="acc%d" % t) for t in range(PACK)]
+        sc_cols = P // BYTES_PER_I32
         for t in range(PACK):
             nc.tensor.matmul_mx(acc[t][:], lhsT=w_st[:, P * t:P * t + P].bitcast(E4M3X4),
-                                lhsT_scale=w_plane[:, 32 * t:32 * t + 32].bitcast(U8),
+                                lhsT_scale=w_sc[:, sc_cols * t:sc_cols * (t + 1)].bitcast(U8),
                                 rhs=xt_w_g[:].bitcast(E2M1X4), rhs_scale=xt_sc_g[:], start=True, stop=False)
         for t in range(PACK):
-            nc.tensor.matmul_mx(acc[t][:], lhsT=w0_st[:, 64 * t:64 * t + 64].bitcast(E2M1X4),
-                                lhsT_scale=w0_planes[:, 0, 32 * t:32 * t + 32].bitcast(U8),
+            nc.tensor.matmul_mx(acc[t][:], lhsT=w0_st[:, P // 2 * t:P // 2 * (t + 1)].bitcast(E2M1X4),
+                                lhsT_scale=w0_sc[:, 0, sc_cols * t:sc_cols * (t + 1)].bitcast(U8),
                                 rhs=xo_w_g[:].bitcast(E4M3X4), rhs_scale=xo_sc_g[:], start=False, stop=True)
 
         turn(sa_rows, sa_t, "sa_ps", nc.scalar.copy)
@@ -158,9 +168,10 @@ def tile_list_codedcolumns_kernel(tc, xt_words, xt_scales, xo_words, xo_scales, 
         hid4 = sb.tile([P, O * PACK], BF16, name="hid4", align_bytes=64)
 
         def weave(copy, dst, src):
-            copy(dst.rearrange("p (c i t) -> p c t i", i=4, t=PACK), src.rearrange("p t (c i) -> p c t i", i=4))
+            copy(dst.rearrange("p (c i t) -> p c t i", i=WEAVE, t=PACK),
+                 src.rearrange("p t (c i) -> p c t i", i=WEAVE))
 
-        weave(nc.scalar.copy, hid4[:, 0:O * PACK // 2], hid[:, :, 0:O // 2])
+        weave(nc.scalar.copy, hid4[:], hid[:])
 
         halves = range(N // P)
         wq4 = [sb.tile([P, P * PACK], BF16, name="wq4_%d" % h, align_bytes=64) for h in halves]
@@ -170,19 +181,16 @@ def tile_list_codedcolumns_kernel(tc, xt_words, xt_scales, xo_words, xo_scales, 
             weave(nc.vector.tensor_copy, wq4[h][:], wq[:, :, P * h:P * h + P])
         for h in halves:
             nc.vector.quantize_mx(wq_w[h][:].bitcast(E4M3X4), wq_sc[h][:], wq4[h][:])
-        weave(nc.vector.tensor_copy, hid4[:, O * PACK // 2:], hid[:, :, O // 2:])
         hid_w = sb.tile([P, O], U32, name="hid_w", align_bytes=64)
         hid_sc = sb.tile([P, O], U8, name="hid_sc", align_bytes=64)
         nc.vector.quantize_mx(hid_w[:].bitcast(E5M2X4), hid_sc[:], hid4[:])
 
+        copies_out = (nc.scalar.copy, nc.vector.tensor_copy)
+        store_queues = (nc.scalar, nc.sync)
         for h in halves:
             prod = psum.tile([P, O], F32, name="prod%d" % h)
             nc.tensor.matmul_mx(prod[:], lhsT=wq_w[h][:].bitcast(E4M3X4), lhsT_scale=wq_sc[h][:],
                                 rhs=hid_w[:].bitcast(E5M2X4), rhs_scale=hid_sc[:], start=True, stop=True)
             res = sb.tile([P, O], F32, name="res%d" % h)
-            if h == 0:
-                nc.scalar.copy(res[:], prod[:])
-                nc.scalar.dma_start(out[P * h:P * h + P, :], res[:])
-            else:
-                nc.vector.tensor_copy(res[:], prod[:])
-                nc.sync.dma_start(out[P * h:P * h + P, :], res[:])
+            copies_out[h](res[:], prod[:])
+            store_queues[h].dma_start(out[P * h:P * h + P, :], res[:])

from contextlib import ExitStack

import concourse.mybir as mybir
from concourse.masks import make_identity

K, T, J, R, F, Z, N, V, O = 512, 1024, 256, 512, 512, 1024, 256, 1024, 128
FLOPS = 2 * R * J * (K + F) + 2 * R * N * O

F32 = mybir.dt.float32
BF16 = mybir.dt.bfloat16
I32 = mybir.dt.int32
U32 = mybir.dt.uint32
U16 = mybir.dt.uint16
U8 = mybir.dt.uint8
FP8 = mybir.dt.float8_e4m3fn
E4M3X4 = mybir.dt.float8_e4m3fn_x4
E5M2X4 = mybir.dt.float8_e5m2_x4
E2M1X4 = mybir.dt.float4_e2m1fn_x4
ACT = mybir.ActivationFunctionType
MULT = mybir.AluOpType.mult

P = 128
HALF = P // 2
QUAD = 32
LIVE = 4
PACK = 4
RUN = 8
BLOCKS = R // (PACK * RUN)
LIST_ROWS = 16
BYTES_PER_I32 = 4
WEAVE = 4


def tile_list_codedcolumns_kernel(tc, xt_words, xt_scales, xo_words, xo_scales, w_words, w_scales,
                                      w0_words, w0_scales, ca, sw, sa, offs, offs2, offs3, offs4, out):
    nc = tc.nc
    with ExitStack() as ctx:
        lists = ctx.enter_context(tc.tile_pool(name="lists", bufs=1))
        sb = ctx.enter_context(tc.tile_pool(name="sb", bufs=1))
        psum = ctx.enter_context(tc.psum_pool(name="psum", bufs=1))

        idx = lists.tile([P, J // LIST_ROWS], U16, name="idx")
        idx2 = lists.tile([P, J // LIST_ROWS], U16, name="idx2")
        idx3 = lists.tile([P, N // LIST_ROWS], U16, name="idx3")
        idx4 = lists.tile([P, O // LIST_ROWS], U16, name="idx4")

        xo_sc = sb.tile([P, Z], U8, name="xo_sc", align_bytes=64)
        xt_sc = sb.tile([P, T], U8, name="xt_sc", align_bytes=64)
        xo_w = sb.tile([P, Z], U32, name="xo_w", align_bytes=64)
        xt_w = sb.tile([P, T], U16, name="xt_w", align_bytes=64)
        w_raw = sb.tile([P, R], U32, name="w_raw", align_bytes=64)
        w0_raw = sb.tile([P, R // 2], U32, name="w0_raw", align_bytes=64)
        wsc_raw = sb.tile([LIVE, 4, R // BYTES_PER_I32], I32, name="wsc_raw", align_bytes=64)
        w0sc_raw = sb.tile([HALF, 2, R // BYTES_PER_I32], U32, name="w0sc_raw", align_bytes=64)
        ca_rows = [sb.tile([P, V], U8, name="ca_rows%d" % t, align_bytes=64) for t in range(PACK)]
        sw_t = sb.tile([P, PACK], F32, name="sw_t")
        sa_t = sb.tile([P, PACK], F32, name="sa_t")
        sa_rows = sb.tile([P, P], F32, name="sa_rows")
        sw_rows = sb.tile([P, P], F32, name="sw_rows")

        xt_raw = sb.tile([HALF, 2, T // BYTES_PER_I32], I32, name="xt_raw", align_bytes=64)
        xo_raw = sb.tile([HALF, 2, Z // BYTES_PER_I32], I32, name="xo_raw", align_bytes=64)
        w_sc = sb.tile([P, R // BYTES_PER_I32], I32, name="w_sc", align_bytes=64)
        w0_sc = sb.tile([P, 2, R // BYTES_PER_I32], U32, name="w0_sc", align_bytes=64)
        ident = sb.tile([P, P], F32, name="ident")

        nc.vector.memset(xt_raw[:], 0)
        nc.vector.memset(xo_raw[:], 0)
        nc.vector.memset(w_sc[:], 0)
        nc.vector.memset(w0_sc[:].bitcast(I32), 0)
        nc.vector.memset(sa_rows[:], 0.0)
        nc.vector.memset(sw_rows[:], 0.0)
        nc.vector.memset(ident[:], 0.0)
        make_identity(nc, ident[:], nomemset=True)

        def load_scale_rows(raw, scales):
            rows = scales[0].bitcast(I32).rearrange("(h c i) x -> c i h x", h=2, c=2)
            for c in range(2):
                nc.sync.dma_start(raw[QUAD * c:QUAD * c + LIVE].bitcast(I32), rows[c])

        nc.sync.dma_start(idx[:], offs)
        nc.sync.dma_start(xt_w[:].bitcast(I32), xt_words[0].bitcast(I32))
        nc.sync.dma_start(idx2[:], offs2)
        nc.sync.dma_start(wsc_raw[:], w_scales[0].bitcast(I32).rearrange("(quad i) x -> i quad x", i=LIVE))
        load_scale_rows(xt_raw, xt_scales)
        nc.sync.dma_start(xo_w[:].bitcast(I32), xo_words[0].rearrange("p n t -> p (n t)").bitcast(I32))
        nc.sync.dma_start(w_raw[:].bitcast(I32), w_words[0].rearrange("p n t -> p (n t)").bitcast(I32))
        load_scale_rows(xo_raw, xo_scales)
        nc.sync.dma_start(w0_raw[:].bitcast(I32), w0_words[0].bitcast(I32))
        load_scale_rows(w0sc_raw, w0_scales)
        nc.sync.dma_start(idx3[:], offs3)
        ca_planes = ca.rearrange("(b t q) v -> t b (q v)", t=PACK, q=RUN)
        for t in range(PACK // 2):
            nc.sync.dma_start(ca_rows[t][:], ca_planes[t])
        nc.sync.dma_start(sa_rows[0:PACK, :], sa.rearrange("(b t q) o -> t b (q o)", t=PACK, q=RUN))
        for t in range(PACK // 2, PACK):
            nc.sync.dma_start(ca_rows[t][:], ca_planes[t])
        nc.sync.dma_start(sw_rows[0:PACK, :], sw.rearrange("(b t q) o -> t b (q o)", t=PACK, q=RUN))
        nc.sync.dma_start(idx4[:], offs4)

        xo_sc_g = sb.tile([P, J], U8, name="xo_sc_g", align_bytes=64)
        xt_sc_g = sb.tile([P, J], U8, name="xt_sc_g", align_bytes=64)
        xo_w_g = sb.tile([P, J], U32, name="xo_w_g", align_bytes=64)
        xt_w_g = sb.tile([P, J], U16, name="xt_w_g", align_bytes=64)

        def spread(window, raw):
            for h in range(2):
                nc.vector.tensor_copy(window[HALF * h:HALF * h + HALF, :].bitcast(I32), raw[:, h, :])

        nc.vector.tensor_copy(xt_w_g[:], xt_w[:].indirect(idx[:]))
        spread(xt_sc, xt_raw)
        nc.vector.tensor_copy(xt_sc_g[:], xt_sc[:].indirect(idx[:]))
        for quad in range(P // QUAD):
            nc.vector.tensor_copy(
                w_sc[QUAD * quad:QUAD * quad + LIVE, :].rearrange("p (t b e) -> p t b e", t=PACK, b=BLOCKS),
                wsc_raw[:, quad, :].rearrange("p (b t e) -> p t b e", t=PACK, b=BLOCKS))
        nc.vector.tensor_copy(xo_w_g[:], xo_w[:].indirect(idx2[:]))
        spread(xo_sc, xo_raw)
        nc.vector.tensor_copy(xo_sc_g[:], xo_sc[:].indirect(idx2[:]))

        def deal_words(words_raw, label):
            words = sb.tile(list(words_raw.shape), U32, name=label, align_bytes=64)
            nc.scalar.copy(words[:].rearrange("p (t b e) -> p t b e", t=PACK, b=BLOCKS),
                           words_raw[:].rearrange("p (b t e) -> p t b e", t=PACK, b=BLOCKS))
            return words

        w_st = deal_words(w_raw, "w_st")
        for c in range(2):
            rows = slice(QUAD * c, QUAD * c + LIVE)
            nc.scalar.copy(w0_sc[rows].rearrange("p h (t b e) -> p h b t e", t=PACK, b=BLOCKS),
                           w0sc_raw[rows].rearrange("p h (b t e) -> p h b t e", t=PACK, b=BLOCKS))
        nc.vector.tensor_copy(w0_sc[HALF:P, 0, :], w0_sc[0:HALF, 1, :])
        w0_st = deal_words(w0_raw, "w0_st")

        def turn(rows, columns, label, copy_out):
            turned = psum.tile([P, P], F32, name=label)
            nc.tensor.transpose(turned[:], rows[:], ident[:])
            copy_out(columns[:], turned[:, 0:PACK])

        acc = [psum.tile([P, J], F32, name="acc%d" % t) for t in range(PACK)]
        sc_cols = P // BYTES_PER_I32
        for t in range(PACK):
            nc.tensor.matmul_mx(acc[t][:], lhsT=w_st[:, P * t:P * t + P].bitcast(E4M3X4),
                                lhsT_scale=w_sc[:, sc_cols * t:sc_cols * (t + 1)].bitcast(U8),
                                rhs=xt_w_g[:].bitcast(E2M1X4), rhs_scale=xt_sc_g[:], start=True, stop=False)
        for t in range(PACK):
            nc.tensor.matmul_mx(acc[t][:], lhsT=w0_st[:, P // 2 * t:P // 2 * (t + 1)].bitcast(E2M1X4),
                                lhsT_scale=w0_sc[:, 0, sc_cols * t:sc_cols * (t + 1)].bitcast(U8),
                                rhs=xo_w_g[:].bitcast(E4M3X4), rhs_scale=xo_sc_g[:], start=False, stop=True)

        turn(sa_rows, sa_t, "sa_ps", nc.scalar.copy)
        turn(sw_rows, sw_t, "sw_ps", nc.vector.tensor_copy)

        codes = sb.tile([P, PACK, N], U8, name="codes", align_bytes=64)
        wq = sb.tile([P, PACK, N], BF16, name="wq", align_bytes=64)
        for t in range(PACK):
            nc.vector.tensor_copy(codes[:, t, :], ca_rows[t][:].indirect(idx3[:]))
        for t in range(PACK):
            nc.vector.tensor_scalar(wq[:, t, :], codes[:, t, :].bitcast(FP8), sw_t[:, t:t + 1], None, MULT)

        hid = sb.tile([P, PACK, O], BF16, name="hid", align_bytes=64)
        g1 = [sb.tile([P, J], F32, name="g1_%d" % t, align_bytes=64) for t in range(PACK)]
        for t in range(PACK):
            nc.scalar.activation(g1[t][:], acc[t][:], ACT.Relu)
        for t in range(PACK):
            nc.scalar.activation(hid[:, t, :], g1[t][:].indirect(idx4[:]), ACT.Copy, scale=sa_t[:, t:t + 1])

        hid4 = sb.tile([P, O * PACK], BF16, name="hid4", align_bytes=64)

        def weave(copy, dst, src):
            copy(dst.rearrange("p (c i t) -> p c t i", i=WEAVE, t=PACK),
                 src.rearrange("p t (c i) -> p c t i", i=WEAVE))

        weave(nc.scalar.copy, hid4[:], hid[:])

        halves = range(N // P)
        wq4 = [sb.tile([P, P * PACK], BF16, name="wq4_%d" % h, align_bytes=64) for h in halves]
        wq_w = [sb.tile([P, P], U32, name="wq_w%d" % h, align_bytes=64) for h in halves]
        wq_sc = [sb.tile([P, P], U8, name="wq_sc%d" % h, align_bytes=64) for h in halves]
        for h in halves:
            weave(nc.vector.tensor_copy, wq4[h][:], wq[:, :, P * h:P * h + P])
        for h in halves:
            nc.vector.quantize_mx(wq_w[h][:].bitcast(E4M3X4), wq_sc[h][:], wq4[h][:])
        hid_w = sb.tile([P, O], U32, name="hid_w", align_bytes=64)
        hid_sc = sb.tile([P, O], U8, name="hid_sc", align_bytes=64)
        nc.vector.quantize_mx(hid_w[:].bitcast(E5M2X4), hid_sc[:], hid4[:])

        copies_out = (nc.scalar.copy, nc.vector.tensor_copy)
        store_queues = (nc.scalar, nc.sync)
        for h in halves:
            prod = psum.tile([P, O], F32, name="prod%d" % h)
            nc.tensor.matmul_mx(prod[:], lhsT=wq_w[h][:].bitcast(E4M3X4), lhsT_scale=wq_sc[h][:],
                                rhs=hid_w[:].bitcast(E5M2X4), rhs_scale=hid_sc[:], start=True, stop=True)
            res = sb.tile([P, O], F32, name="res%d" % h)
            copies_out[h](res[:], prod[:])
            store_queues[h].dma_start(out[P * h:P * h + P, :], res[:])
